import numpy as np
import ml_dtypes


def mxq(x, axis, fmt="e4m3"):
    dtype, down = {"e4m3": (ml_dtypes.float8_e4m3fn, 7), "e5m2": (ml_dtypes.float8_e5m2, 14)}[fmt]
    v = np.moveaxis(np.asarray(x, np.float32).astype(ml_dtypes.bfloat16).astype(np.float64), axis, -1)
    blocks = v.reshape(v.shape[:-1] + (-1, 32))
    amax = np.abs(blocks).max(-1, keepdims=True)
    byte = np.maximum(np.where(amax > 0, np.frexp(amax)[1] - 1 + 127, 0) - down, 1)
    scale = np.exp2(byte - 127.0)
    codes = (blocks / scale).astype(np.float32).astype(dtype).astype(np.float64)
    return np.moveaxis((codes * scale).reshape(v.shape), -1, axis)


WIDE = False


def mx_kscale(k):
    if not WIDE:
        return np.ones(k)
    levels = np.array([10, -10, 5, -5, 0])
    if k % 512:
        return np.exp2(np.random.permutation(np.resize(levels, k // 32))).repeat(32)
    a = np.empty((k // 512, 16))
    for p in range(k // 512):
        a[p, :8] = np.random.permutation(np.resize(levels, 8))
        for g in range(8):
            far = levels[np.abs(levels - a[p, g]) >= 10]
            a[p, g + 8] = far[np.random.randint(len(far))]
    return np.exp2(a.ravel()).repeat(32)


def f64(x):
    return np.asarray(x).astype(np.float64)


def striped(idx):
    return np.tile(idx.reshape(-1, 16).T, (8, 1)).astype(np.uint16)


def unstriped(offs):
    return offs[:16].T.reshape(-1).astype(np.int64)


def pack_weight(w):
    k, n = w.shape
    w = f64(np.asarray(w, np.float32).astype(ml_dtypes.bfloat16)).reshape(k // 32, 32, n)
    amax = np.abs(w).max(1)
    byte = np.clip(np.where(amax > 0, np.frexp(amax)[1] - 1 + 127 - 7, 1), 1, 254)
    scaled = (w * np.exp2(127.0 - byte)[:, None, :]).reshape(k, n).astype(np.float32)
    words = np.ascontiguousarray(scaled.reshape(k // 512, 128, 4, n).transpose(0, 1, 3, 2)).astype(ml_dtypes.float8_e4m3fn).view(np.uint8)
    return words, np.ascontiguousarray(byte.astype(np.uint8).reshape(k // 512, 16, n))


def unpack_weight(words, scales):
    g, p, n, _ = words.shape
    vals = np.ascontiguousarray(words).view(ml_dtypes.float8_e4m3fn).astype(np.float64) * np.repeat(np.exp2(scales.astype(np.float64) - 127.0), 8, axis=1)[..., None]
    return vals.transpose(0, 1, 3, 2).reshape(g * 512, n)


K, T, D, S, V, N = 512, 2048, 4, 2048, 512, 256


def setup_inputs():
    n = np.random.standard_normal
    s = mx_kscale(K)[:, None]
    words, scales = pack_weight(n((K, N)) / np.sqrt(K) / s)
    return {
        "xT": (n((K, T)) * s / np.sqrt(D)).astype(ml_dtypes.bfloat16).astype(np.float32),
        "w_words": words,
        "w_scales": scales,
        "offs": striped(np.concatenate([np.random.permutation(T)[:V] for _ in range(D)])),
    }


def reference(xT, w_words, w_scales, offs):
    w = unpack_weight(w_words, w_scales)
    idx = unstriped(offs)
    x = sum(f64(xT)[:, idx[d * V:(d + 1) * V]] for d in range(D))
    return w.T @ mxq(x, 0, "e4m3")

@@ -1,0 +1,296 @@
+from contextlib import ExitStack
+
+import concourse.mybir as mybir
+from concourse.masks import make_identity
+
+K, T, D, V, N = 512, 2048, 4, 512, 256
+FLOPS = 2 * K * N * V
+
+F32 = mybir.dt.float32
+BF16 = mybir.dt.bfloat16
+I32 = mybir.dt.int32
+U32 = mybir.dt.uint32
+U16 = mybir.dt.uint16
+U8 = mybir.dt.uint8
+FP8X4 = mybir.dt.float8_e4m3fn_x4
+COPY = mybir.ActivationFunctionType.Copy
+MULT = mybir.AluOpType.mult
+ADD = mybir.AluOpType.add
+
+P = 128
+PACK = 4
+HALF = V // 2
+BLOCKS = V // P
+
+LOADS = (((0, 1024), (1024, 2048)), ((0, 1024), (1024, 2048)), ((0, 1024), (1024, 2048)), ((0, 1024), (1024, 2048)))
+STEPS = (
+    ("cast", "V", 0, 0, 1024),
+    ("cast", "V", 0, 1024, 1728),
+    ("cast", "S", 0, 1728, 2048),
+    ("gather", "V", 0, 0, 0, 512, 0),
+    ("add", 0, 0, 0),
+    ("add", 0, 0, 1),
+    ("add", 0, 0, 2),
+    ("add", 0, 0, 3),
+    ("gather", "S", 0, 1, 0, 512, 0),
+    ("add", 0, 1, 0),
+    ("add", 0, 1, 1),
+    ("add", 0, 1, 2),
+    ("add", 0, 1, 3),
+    ("gather", "V", 0, 2, 0, 256, 0),
+    ("add", 0, 2, 0),
+    ("add", 0, 2, 1),
+    ("gather", "S", 0, 3, 0, 512, 2),
+    ("add", 0, 3, 0),
+    ("add", 0, 3, 1),
+    ("add", 0, 3, 2),
+    ("add", 0, 3, 3),
+    ("gather", "S", 0, 2, 256, 512, 4),
+    ("add", 0, 2, 2),
+    ("add", 0, 2, 3),
+    ("cast", "G", 1, 0, 1024),
+    ("cast", "G", 1, 1024, 2048),
+    ("gather", "V", 1, 0, 0, 512, 0),
+    ("add", 1, 0, 0),
+    ("add", 1, 0, 1),
+    ("add", 1, 0, 2),
+    ("add", 1, 0, 3),
+    ("gather", "V", 1, 1, 0, 512, 0),
+    ("add", 1, 1, 0),
+    ("add", 1, 1, 1),
+    ("add", 1, 1, 2),
+    ("add", 1, 1, 3),
+    ("gather", "S", 1, 2, 0, 512, 5),
+    ("add", 1, 2, 0),
+    ("add", 1, 2, 1),
+    ("add", 1, 2, 2),
+    ("add", 1, 2, 3),
+    ("gather", "S", 1, 3, 0, 512, 7),
+    ("add", 1, 3, 0),
+    ("add", 1, 3, 1),
+    ("add", 1, 3, 2),
+    ("add", 1, 3, 3),
+    ("cast", "G", 2, 0, 1024),
+    ("cast", "G", 2, 1024, 2048),
+    ("gather", "V", 2, 0, 0, 512, 0),
+    ("add", 2, 0, 0),
+    ("add", 2, 0, 1),
+    ("add", 2, 0, 2),
+    ("add", 2, 0, 3),
+    ("gather", "V", 2, 1, 0, 512, 0),
+    ("add", 2, 1, 0),
+    ("add", 2, 1, 1),
+    ("add", 2, 1, 2),
+    ("add", 2, 1, 3),
+    ("gather", "S", 2, 2, 0, 512, 0),
+    ("add", 2, 2, 0),
+    ("add", 2, 2, 1),
+    ("add", 2, 2, 2),
+    ("add", 2, 2, 3),
+    ("round", "V", 0, 0),
+    ("round", "V", 0, 1),
+    ("round", "S", 0, 2),
+    ("round", "S", 0, 3),
+    ("gather", "S", 2, 3, 0, 512, 2),
+    ("add", 2, 3, 0),
+    ("add", 2, 3, 1),
+    ("add", 2, 3, 2),
+    ("add", 2, 3, 3),
+    ("cast", "G", 3, 0, 1024),
+    ("cast", "G", 3, 1024, 2048),
+    ("back", 0, 0),
+    ("back", 0, 1),
+    ("back", 0, 2),
+    ("back", 0, 3),
+    ("gather", "V", 3, 0, 0, 256, 0),
+    ("add", 3, 0, 0),
+    ("add", 3, 0, 1),
+    ("gather", "V", 3, 1, 0, 256, 0),
+    ("add", 3, 1, 0),
+    ("add", 3, 1, 1),
+    ("gather", "V", 3, 2, 0, 256, 0),
+    ("add", 3, 2, 0),
+    ("add", 3, 2, 1),
+    ("gather", "S", 3, 3, 0, 256, 4),
+    ("add", 3, 3, 0),
+    ("add", 3, 3, 1),
+    ("gather", "V", 3, 0, 256, 512, 0),
+    ("add", 3, 0, 2),
+    ("add", 3, 0, 3),
+    ("gather", "S", 3, 2, 256, 512, 5),
+    ("add", 3, 2, 2),
+    ("add", 3, 2, 3),
+    ("round", "S", 1, 0),
+    ("round", "S", 1, 1),
+    ("back", 1, 0),
+    ("back", 1, 1),
+    ("gather", "V", 3, 1, 256, 512, 0),
+    ("add", 3, 1, 2),
+    ("add", 3, 1, 3),
+    ("gather", "V", 3, 3, 256, 512, 0),
+    ("add", 3, 3, 2),
+    ("add", 3, 3, 3),
+    ("inter", "S", 0),
+    ("inter", "S", 1),
+    ("quant", 0),
+    ("mul", 0, 0),
+    ("mul", 0, 1),
+    ("round", "S", 1, 2),
+    ("round", "V", 1, 3),
+    ("back", 1, 2),
+    ("back", 1, 3),
+    ("leave", "S", 0, 0, "sync"),
+    ("leave", "V", 0, 1, "sync"),
+    ("inter", "S", 2),
+    ("inter", "V", 3),
+    ("quant", 1),
+    ("mul", 1, 0),
+    ("mul", 1, 1),
+    ("leave", "S", 1, 0, "scalar"),
+    ("leave", "V", 1, 1, "sync"),
+)
+RING = 9
+RING_V = 4
+
+
+def tile_picked_hash_lin_none_sub_l_kernel(tc, xT, w_words, w_scales, offs, out):
+    nc = tc.nc
+    with ExitStack() as ctx:
+        keep = ctx.enter_context(tc.tile_pool(name="keep", bufs=1))
+        psum = ctx.enter_context(tc.psum_pool(name="psum", bufs=1))
+
+        offsets = keep.tile([P, D * V // 16], U16, name="offsets")
+        table = [keep.tile([P, T], F32, name=f"table{t}") for t in range(PACK)]
+        table16 = [keep.tile([P, T], BF16, name=f"table16_{t}") for t in range(PACK)]
+        picked = [[keep.tile([P, V], F32, name=f"picked{t}_{d}") for d in range(D)] for t in range(PACK)]
+        spaced = keep.tile([P, RING * HALF], F32, name="spaced")
+        source = {}
+        w_codes = keep.tile([P, N], U32, name="w_codes", align_bytes=64)
+        w_scale = keep.tile([P, N], U8, name="w_scale", align_bytes=64)
+        ident = keep.tile([P, P], F32, name="ident")
+        warm = keep.tile([P, 8], F32, name="warm")
+        warm_out = keep.tile([P, 8], F32, name="warm_out")
+        sums16 = [[keep.tile([P, 2 * P], BF16, name=f"sums16_{u}_{b}") for b in range(BLOCKS)] for u in range(2)]
+        x16 = [keep.tile([P, PACK * HALF], BF16, name=f"x16_{h}", align_bytes=64) for h in range(2)]
+        x_codes = [keep.tile([P, HALF], U32, name=f"x_codes{h}", align_bytes=64) for h in range(2)]
+        x_scale = [keep.tile([P, HALF], U8, name=f"x_scale{h}", align_bytes=64) for h in range(2)]
+        result = [[keep.tile([P, HALF], F32, name=f"result{h}_{m}") for m in range(2)] for h in range(2)]
+        bank = [[psum.tile([P, 4 * P], F32, name=f"bank{u}_{b}") for b in range(BLOCKS)] for u in range(2)]
+
+        rows = xT.rearrange("(p t) c -> p t c", t=PACK)
+        for t in range(PACK):
+            for lo, hi in LOADS[t]:
+                nc.sync.dma_start(out=table[t][:, lo:hi], in_=rows[:, t, lo:hi])
+                if t == 0 and lo == 0:
+                    nc.sync.dma_start(offsets[:], offs)
+
+        nc.vector.memset(warm[:], 0.0)
+        nc.scalar.activation(warm_out[:], warm[:], COPY)
+        make_identity(nc, ident[:])
+        nc.vector.memset(w_scale[:].bitcast(U32), 0)
+        nc.sync.dma_start(
+            out=w_codes[:].bitcast(I32), in_=w_words[0].rearrange("p n t -> p (n t)").bitcast(I32)
+        )
+        for q in range(4):
+            nc.sync.dma_start(
+                out=w_scale[32 * q : 32 * q + 4, :].bitcast(I32), in_=w_scales[0, 4 * q : 4 * q + 4, :].bitcast(I32)
+            )
+        nc.vector.memset(spaced[:, : RING_V * HALF], 0.0)
+        nc.gpsimd.memset(spaced[:, RING_V * HALF :], 0.0)
+
+        seen = {}
+
+        def cast(eng, t, lo, hi):
+            if eng == "V":
+                nc.vector.tensor_copy(table16[t][:, lo:hi], table[t][:, lo:hi])
+            elif eng == "S":
+                nc.scalar.activation(table16[t][:, lo:hi], table[t][:, lo:hi], COPY)
+            else:
+                nc.gpsimd.tensor_scalar(table16[t][:, lo:hi], table[t][:, lo:hi], 1.0, 0.0, MULT, ADD)
+
+        def gather(eng, t, d, lo, hi, slot):
+            piece = offsets[:, (d * V + lo) // 16 : (d * V + hi) // 16]
+            if eng == "V":
+                nc.vector.tensor_copy(picked[t][d][:, lo:hi], table[t][:].indirect(piece))
+                for b in range(lo // P, hi // P):
+                    source[(t, d, b)] = picked[t][d][:, b * P : (b + 1) * P]
+            else:
+                first = slot * HALF - lo
+                upper = spaced[:, first + lo : first + hi].bitcast(BF16)[:, 1::2]
+                nc.scalar.activation(upper, table16[t][:].indirect(piece), COPY)
+                for b in range(lo // P, hi // P):
+                    source[(t, d, b)] = spaced[:, first + b * P : first + (b + 1) * P]
+
+        def add(t, d, b):
+            count = seen.get((t, b), 0)
+            seen.setdefault((t, b), 0)
+            seen[(t, b)] = count + 1
+            e = t % 2
+            nc.tensor.matmul(
+                bank[t // 2][b][:, e * P : (e + 1) * P],
+                lhsT=source[(t, d, b)],
+                rhs=ident[:],
+                start=(count == 0),
+                stop=(count == D - 1),
+                is_transpose=True,
+            )
+
+        def copy(eng, dst, src):
+            if eng == "V":
+                nc.vector.tensor_copy(dst, src)
+            else:
+                nc.scalar.copy(dst, src)
+
+        def round_sums(eng, u, b):
+            copy(
+                eng,
+                sums16[u][b][:].rearrange("v (p e) -> v p e", e=2),
+                bank[u][b][:, : 2 * P].rearrange("v (e p) -> v p e", e=2),
+            )
+
+        def turn_back(u, b):
+            nc.tensor.transpose(bank[0][b][:, (2 + u) * P : (3 + u) * P], sums16[u][b][:].bitcast(F32), ident[:])
+
+        def interleave(eng, b):
+            h, c = divmod(b, 2)
+            copy(
+                eng,
+                x16[h][:, c * PACK * P : (c + 1) * PACK * P].bitcast(F32).rearrange("p (v u) -> p v u", u=2),
+                bank[0][b][:, 2 * P :].rearrange("p (u v) -> p v u", u=2),
+            )
+
+        def quantize(h):
+            nc.vector.quantize_mx(out=x_codes[h][:].bitcast(FP8X4), scales=x_scale[h][:], in_=x16[h][:])
+
+        def multiply(h, m):
+            nc.tensor.matmul_mx(
+                out=bank[1][2 * h + m][:, 2 * P :],
+                lhsT=w_codes[:, m * P : (m + 1) * P].bitcast(FP8X4),
+                lhsT_scale=w_scale[:, m * P : (m + 1) * P],
+                rhs=x_codes[h][:].bitcast(FP8X4),
+                rhs_scale=x_scale[h][:],
+                start=True,
+                stop=True,
+            )
+
+        def leave(eng, h, m, queue):
+            copy(eng, result[h][m][:], bank[1][2 * h + m][:, 2 * P :])
+            dst = out[m * P : (m + 1) * P, h * HALF : (h + 1) * HALF]
+            if queue == "sync":
+                nc.sync.dma_start(out=dst, in_=result[h][m][:])
+            else:
+                nc.scalar.dma_start(out=dst, in_=result[h][m][:])
+
+        calls = {
+            "cast": cast,
+            "gather": gather,
+            "add": add,
+            "round": round_sums,
+            "back": turn_back,
+            "inter": interleave,
+            "quant": quantize,
+            "mul": multiply,
+            "leave": leave,
+        }
+        for step in STEPS:
+            calls[step[0]](*step[1:])

@@ -22,135 +22,137 @@ PACK = 4
 HALF = V // 2
 BLOCKS = V // P
 
-LOADS = (((0, 1024), (1024, 2048)), ((0, 1024), (1024, 2048)), ((0, 1024), (1024, 2048)), ((0, 1024), (1024, 2048)))
+LOADS = (((0, 1024), (1024, 1792), (1792, 2048)), ((0, 1024), (1024, 2048)), ((0, 1024), (1024, 2048)), ((0, 1024), (1024, 2048)))
 STEPS = (
     ("cast", "V", 0, 0, 1024),
-    ("cast", "V", 0, 1024, 1728),
-    ("cast", "S", 0, 1728, 2048),
+    ("cast", "V", 0, 1024, 1792),
+    ("cast", "S", 0, 1792, 2048),
+    ("gather", "V", 0, 1, 0, 512, 0),
+    ("gather", "S", 0, 3, 0, 512, 0),
+    ("cast", "G", 2, 0, 1024),
     ("gather", "V", 0, 0, 0, 512, 0),
-    ("add", 0, 0, 0),
-    ("add", 0, 0, 1),
-    ("add", 0, 0, 2),
-    ("add", 0, 0, 3),
-    ("gather", "S", 0, 1, 0, 512, 0),
     ("add", 0, 1, 0),
     ("add", 0, 1, 1),
+    ("gather", "S", 0, 2, 0, 512, 2),
     ("add", 0, 1, 2),
     ("add", 0, 1, 3),
-    ("gather", "V", 0, 2, 0, 256, 0),
+    ("gather", "V", 2, 3, 0, 512, 0),
+    ("cast", "G", 2, 1536, 2048),
     ("add", 0, 2, 0),
-    ("add", 0, 2, 1),
-    ("gather", "S", 0, 3, 0, 512, 2),
     ("add", 0, 3, 0),
+    ("add", 0, 2, 1),
+    ("cast", "G", 2, 1024, 1536),
     ("add", 0, 3, 1),
-    ("add", 0, 3, 2),
-    ("add", 0, 3, 3),
-    ("gather", "S", 0, 2, 256, 512, 4),
+    ("cast", "S", 1, 0, 1024),
+    ("gather", "V", 2, 2, 0, 512, 0),
     ("add", 0, 2, 2),
+    ("add", 0, 3, 2),
     ("add", 0, 2, 3),
-    ("cast", "G", 1, 0, 1024),
-    ("cast", "G", 1, 1024, 2048),
-    ("gather", "V", 1, 0, 0, 512, 0),
-    ("add", 1, 0, 0),
-    ("add", 1, 0, 1),
-    ("add", 1, 0, 2),
-    ("add", 1, 0, 3),
-    ("gather", "V", 1, 1, 0, 512, 0),
-    ("add", 1, 1, 0),
-    ("add", 1, 1, 1),
-    ("add", 1, 1, 2),
-    ("add", 1, 1, 3),
-    ("gather", "S", 1, 2, 0, 512, 5),
-    ("add", 1, 2, 0),
-    ("add", 1, 2, 1),
-    ("add", 1, 2, 2),
-    ("add", 1, 2, 3),
-    ("gather", "S", 1, 3, 0, 512, 7),
-    ("add", 1, 3, 0),
-    ("add", 1, 3, 1),
-    ("add", 1, 3, 2),
-    ("add", 1, 3, 3),
-    ("cast", "G", 2, 0, 1024),
-    ("cast", "G", 2, 1024, 2048),
-    ("gather", "V", 2, 0, 0, 512, 0),
-    ("add", 2, 0, 0),
-    ("add", 2, 0, 1),
-    ("add", 2, 0, 2),
-    ("add", 2, 0, 3),
-    ("gather", "V", 2, 1, 0, 512, 0),
-    ("add", 2, 1, 0),
-    ("add", 2, 1, 1),
-    ("add", 2, 1, 2),
-    ("add", 2, 1, 3),
-    ("gather", "S", 2, 2, 0, 512, 0),
-    ("add", 2, 2, 0),
-    ("add", 2, 2, 1),
-    ("add", 2, 2, 2),
-    ("add", 2, 2, 3),
-    ("round", "V", 0, 0),
-    ("round", "V", 0, 1),
-    ("round", "S", 0, 2),
-    ("round", "S", 0, 3),
-    ("gather", "S", 2, 3, 0, 512, 2),
+    ("add", 0, 3, 3),
     ("add", 2, 3, 0),
     ("add", 2, 3, 1),
     ("add", 2, 3, 2),
     ("add", 2, 3, 3),
+    ("gather", "S", 2, 0, 0, 512, 4),
+    ("cast", "G", 1, 1024, 1536),
+    ("add", 0, 0, 0),
+    ("gather", "V", 1, 0, 0, 512, 0),
+    ("add", 0, 0, 1),
+    ("add", 0, 0, 2),
+    ("add", 0, 0, 3),
+    ("add", 2, 2, 0),
+    ("add", 2, 2, 1),
+    ("cast", "G", 1, 1536, 2048),
+    ("add", 2, 2, 2),
+    ("add", 2, 2, 3),
+    ("gather", "S", 2, 1, 0, 512, 6),
+    ("gather", "V", 1, 2, 0, 512, 0),
+    ("add", 2, 0, 0),
+    ("add", 2, 0, 1),
     ("cast", "G", 3, 0, 1024),
-    ("cast", "G", 3, 1024, 2048),
-    ("back", 0, 0),
-    ("back", 0, 1),
-    ("back", 0, 2),
-    ("back", 0, 3),
-    ("gather", "V", 3, 0, 0, 256, 0),
-    ("add", 3, 0, 0),
-    ("add", 3, 0, 1),
-    ("gather", "V", 3, 1, 0, 256, 0),
-    ("add", 3, 1, 0),
-    ("add", 3, 1, 1),
-    ("gather", "V", 3, 2, 0, 256, 0),
-    ("add", 3, 2, 0),
-    ("add", 3, 2, 1),
-    ("gather", "S", 3, 3, 0, 256, 4),
+    ("add", 2, 0, 2),
+    ("add", 2, 0, 3),
+    ("add", 1, 0, 0),
+    ("add", 1, 0, 1),
+    ("add", 1, 0, 2),
+    ("gather", "S", 1, 3, 0, 256, 8),
+    ("add", 1, 0, 3),
+    ("gather", "V", 3, 3, 0, 512, 0),
+    ("add", 2, 1, 0),
+    ("add", 2, 1, 1),
+    ("add", 2, 1, 2),
+    ("gather", "S", 1, 1, 0, 256, 9),
+    ("add", 2, 1, 3),
+    ("cast", "G", 3, 1536, 2048),
+    ("add", 1, 2, 0),
+    ("add", 1, 2, 1),
+    ("add", 1, 2, 2),
+    ("add", 1, 2, 3),
+    ("gather", "V", 3, 1, 0, 512, 0),
+    ("gather", "S", 1, 1, 256, 512, 0),
+    ("add", 1, 3, 0),
+    ("cast", "G", 3, 1024, 1536),
+    ("add", 1, 3, 1),
+    ("add", 1, 1, 0),
+    ("add", 1, 1, 1),
+    ("gather", "S", 1, 3, 256, 512, 1),
     ("add", 3, 3, 0),
     ("add", 3, 3, 1),
-    ("gather", "V", 3, 0, 256, 512, 0),
-    ("add", 3, 0, 2),
-    ("add", 3, 0, 3),
-    ("gather", "S", 3, 2, 256, 512, 5),
-    ("add", 3, 2, 2),
-    ("add", 3, 2, 3),
-    ("round", "S", 1, 0),
-    ("round", "S", 1, 1),
-    ("back", 1, 0),
-    ("back", 1, 1),
-    ("gather", "V", 3, 1, 256, 512, 0),
-    ("add", 3, 1, 2),
-    ("add", 3, 1, 3),
-    ("gather", "V", 3, 3, 256, 512, 0),
     ("add", 3, 3, 2),
     ("add", 3, 3, 3),
-    ("inter", "S", 0),
-    ("inter", "S", 1),
-    ("quant", 0),
-    ("mul", 0, 0),
-    ("mul", 0, 1),
+    ("gather", "V", 3, 2, 256, 512, 0),
+    ("add", 1, 1, 2),
+    ("gather", "S", 3, 0, 256, 512, 2),
+    ("add", 1, 1, 3),
+    ("add", 1, 3, 2),
+    ("add", 1, 3, 3),
+    ("gather", "V", 3, 2, 0, 256, 0),
+    ("add", 3, 1, 0),
+    ("gather", "S", 3, 0, 0, 256, 3),
+    ("add", 3, 1, 1),
+    ("add", 3, 1, 2),
+    ("add", 3, 1, 3),
+    ("add", 3, 0, 2),
+    ("round", "V", 0, 1),
+    ("add", 3, 0, 3),
+    ("round", "S", 0, 3),
+    ("add", 3, 2, 2),
+    ("add", 3, 2, 3),
+    ("round", "S", 0, 2),
+    ("add", 3, 0, 0),
+    ("add", 3, 0, 1),
+    ("add", 3, 2, 0),
     ("round", "S", 1, 2),
     ("round", "V", 1, 3),
-    ("back", 1, 2),
+    ("add", 3, 2, 1),
+    ("back", 0, 3),
+    ("back", 0, 2),
+    ("round", "V", 0, 0),
+    ("round", "S", 1, 0),
     ("back", 1, 3),
-    ("leave", "S", 0, 0, "sync"),
-    ("leave", "V", 0, 1, "sync"),
-    ("inter", "S", 2),
-    ("inter", "V", 3),
+    ("round", "V", 1, 1),
+    ("back", 1, 2),
+    ("back", 0, 0),
+    ("back", 1, 0),
+    ("inter", "S", 3),
+    ("back", 1, 1),
+    ("inter", "V", 2),
+    ("back", 0, 1),
+    ("inter", "S", 0),
     ("quant", 1),
-    ("mul", 1, 0),
+    ("inter", "S", 1),
     ("mul", 1, 1),
-    ("leave", "S", 1, 0, "scalar"),
+    ("quant", 0),
+    ("mul", 1, 0),
+    ("mul", 0, 1),
     ("leave", "V", 1, 1, "sync"),
+    ("mul", 0, 0),
+    ("leave", "V", 1, 0, "sync"),
+    ("leave", "V", 0, 1, "sync"),
+    ("leave", "S", 0, 0, "scalar"),
 )
-RING = 9
-RING_V = 4
+RING = 10
+RING_V = 2
 
 
 def tile_picked_hash_lin_none_sub_l_kernel(tc, xT, w_words, w_scales, offs, out):
@@ -165,6 +167,7 @@ def tile_picked_hash_lin_none_sub_l_kernel(tc, xT, w_words, w_scales, offs, out)
         picked = [[keep.tile([P, V], F32, name=f"picked{t}_{d}") for d in range(D)] for t in range(PACK)]
         spaced = keep.tile([P, RING * HALF], F32, name="spaced")
         source = {}
+        whole = {}
         w_codes = keep.tile([P, N], U32, name="w_codes", align_bytes=64)
         w_scale = keep.tile([P, N], U8, name="w_scale", align_bytes=64)
         ident = keep.tile([P, P], F32, name="ident")
@@ -178,7 +181,7 @@ def tile_picked_hash_lin_none_sub_l_kernel(tc, xT, w_words, w_scales, offs, out)
         bank = [[psum.tile([P, 4 * P], F32, name=f"bank{u}_{b}") for b in range(BLOCKS)] for u in range(2)]
 
         rows = xT.rearrange("(p t) c -> p t c", t=PACK)
-        for t in range(PACK):
+        for t in (0, 2, 1, 3):
             for lo, hi in LOADS[t]:
                 nc.sync.dma_start(out=table[t][:, lo:hi], in_=rows[:, t, lo:hi])
                 if t == 0 and lo == 0:
@@ -214,12 +217,22 @@ def tile_picked_hash_lin_none_sub_l_kernel(tc, xT, w_words, w_scales, offs, out)
                 nc.vector.tensor_copy(picked[t][d][:, lo:hi], table[t][:].indirect(piece))
                 for b in range(lo // P, hi // P):
                     source[(t, d, b)] = picked[t][d][:, b * P : (b + 1) * P]
+                for c in range(lo, hi, HALF):
+                    whole[(t, d, c)] = picked[t][d][:, c : c + HALF]
             else:
                 first = slot * HALF - lo
                 upper = spaced[:, first + lo : first + hi].bitcast(BF16)[:, 1::2]
                 nc.scalar.activation(upper, table16[t][:].indirect(piece), COPY)
                 for b in range(lo // P, hi // P):
                     source[(t, d, b)] = spaced[:, first + b * P : first + (b + 1) * P]
+                for c in range(lo, hi, HALF):
+                    whole[(t, d, c)] = spaced[:, first + c : first + c + HALF]
+
+        def pre(eng, t, d0, d1, lo, hi):
+            both = keep.tile([P, hi - lo], F32, name=f"both{t}_{d0}_{lo}")
+            nc.vector.tensor_tensor(both[:], whole[(t, d0, lo)], whole[(t, d1, lo)], ADD)
+            for b in range(lo // P, hi // P):
+                source[(t, f"{d0}+", b)] = both[:, b * P - lo : (b + 1) * P - lo]
 
         def add(t, d, b):
             count = seen.get((t, b), 0)
@@ -231,7 +244,7 @@ def tile_picked_hash_lin_none_sub_l_kernel(tc, xT, w_words, w_scales, offs, out)
                 lhsT=source[(t, d, b)],
                 rhs=ident[:],
                 start=(count == 0),
-                stop=(count == D - 1),
+                stop=(count == len([s for s in STEPS if s[0] == "add" and s[1] == t and s[3] == b]) - 1),
                 is_transpose=True,
             )
 
@@ -285,6 +298,7 @@ def tile_picked_hash_lin_none_sub_l_kernel(tc, xT, w_words, w_scales, offs, out)
             "cast": cast,
             "gather": gather,
             "add": add,
+            "pre": pre,
             "round": round_sums,
             "back": turn_back,
             "inter": interleave,

from contextlib import ExitStack

import concourse.mybir as mybir
from concourse.masks import make_identity

K, T, D, V, N = 512, 2048, 4, 512, 256
FLOPS = 2 * K * N * V

F32 = mybir.dt.float32
BF16 = mybir.dt.bfloat16
I32 = mybir.dt.int32
U32 = mybir.dt.uint32
U16 = mybir.dt.uint16
U8 = mybir.dt.uint8
FP8X4 = mybir.dt.float8_e4m3fn_x4
COPY = mybir.ActivationFunctionType.Copy
MULT = mybir.AluOpType.mult
ADD = mybir.AluOpType.add

P = 128
PACK = 4
HALF = V // 2
BLOCKS = V // P

LOADS = (((0, 1024), (1024, 1792), (1792, 2048)), ((0, 1024), (1024, 2048)), ((0, 1024), (1024, 2048)), ((0, 1024), (1024, 2048)))
STEPS = (
    ("cast", "V", 0, 0, 1024),
    ("cast", "V", 0, 1024, 1792),
    ("cast", "S", 0, 1792, 2048),
    ("gather", "V", 0, 1, 0, 512, 0),
    ("gather", "S", 0, 3, 0, 512, 0),
    ("cast", "G", 2, 0, 1024),
    ("gather", "V", 0, 0, 0, 512, 0),
    ("add", 0, 1, 0),
    ("add", 0, 1, 1),
    ("gather", "S", 0, 2, 0, 512, 2),
    ("add", 0, 1, 2),
    ("add", 0, 1, 3),
    ("gather", "V", 2, 3, 0, 512, 0),
    ("cast", "G", 2, 1536, 2048),
    ("add", 0, 2, 0),
    ("add", 0, 3, 0),
    ("add", 0, 2, 1),
    ("cast", "G", 2, 1024, 1536),
    ("add", 0, 3, 1),
    ("cast", "S", 1, 0, 1024),
    ("gather", "V", 2, 2, 0, 512, 0),
    ("add", 0, 2, 2),
    ("add", 0, 3, 2),
    ("add", 0, 2, 3),
    ("add", 0, 3, 3),
    ("add", 2, 3, 0),
    ("add", 2, 3, 1),
    ("add", 2, 3, 2),
    ("add", 2, 3, 3),
    ("gather", "S", 2, 0, 0, 512, 4),
    ("cast", "G", 1, 1024, 1536),
    ("add", 0, 0, 0),
    ("gather", "V", 1, 0, 0, 512, 0),
    ("add", 0, 0, 1),
    ("add", 0, 0, 2),
    ("add", 0, 0, 3),
    ("add", 2, 2, 0),
    ("add", 2, 2, 1),
    ("cast", "G", 1, 1536, 2048),
    ("add", 2, 2, 2),
    ("add", 2, 2, 3),
    ("gather", "S", 2, 1, 0, 512, 6),
    ("gather", "V", 1, 2, 0, 512, 0),
    ("add", 2, 0, 0),
    ("add", 2, 0, 1),
    ("cast", "G", 3, 0, 1024),
    ("add", 2, 0, 2),
    ("add", 2, 0, 3),
    ("add", 1, 0, 0),
    ("add", 1, 0, 1),
    ("add", 1, 0, 2),
    ("gather", "S", 1, 3, 0, 256, 8),
    ("add", 1, 0, 3),
    ("gather", "V", 3, 3, 0, 512, 0),
    ("add", 2, 1, 0),
    ("add", 2, 1, 1),
    ("add", 2, 1, 2),
    ("gather", "S", 1, 1, 0, 256, 9),
    ("add", 2, 1, 3),
    ("cast", "G", 3, 1536, 2048),
    ("add", 1, 2, 0),
    ("add", 1, 2, 1),
    ("add", 1, 2, 2),
    ("add", 1, 2, 3),
    ("gather", "V", 3, 1, 0, 512, 0),
    ("gather", "S", 1, 1, 256, 512, 0),
    ("add", 1, 3, 0),
    ("cast", "G", 3, 1024, 1536),
    ("add", 1, 3, 1),
    ("add", 1, 1, 0),
    ("add", 1, 1, 1),
    ("gather", "S", 1, 3, 256, 512, 1),
    ("add", 3, 3, 0),
    ("add", 3, 3, 1),
    ("add", 3, 3, 2),
    ("add", 3, 3, 3),
    ("gather", "V", 3, 2, 256, 512, 0),
    ("add", 1, 1, 2),
    ("gather", "S", 3, 0, 256, 512, 2),
    ("add", 1, 1, 3),
    ("add", 1, 3, 2),
    ("add", 1, 3, 3),
    ("gather", "V", 3, 2, 0, 256, 0),
    ("add", 3, 1, 0),
    ("gather", "S", 3, 0, 0, 256, 3),
    ("add", 3, 1, 1),
    ("add", 3, 1, 2),
    ("add", 3, 1, 3),
    ("add", 3, 0, 2),
    ("round", "V", 0, 1),
    ("add", 3, 0, 3),
    ("round", "S", 0, 3),
    ("add", 3, 2, 2),
    ("add", 3, 2, 3),
    ("round", "S", 0, 2),
    ("add", 3, 0, 0),
    ("add", 3, 0, 1),
    ("add", 3, 2, 0),
    ("round", "S", 1, 2),
    ("round", "V", 1, 3),
    ("add", 3, 2, 1),
    ("back", 0, 3),
    ("back", 0, 2),
    ("round", "V", 0, 0),
    ("round", "S", 1, 0),
    ("back", 1, 3),
    ("round", "V", 1, 1),
    ("back", 1, 2),
    ("back", 0, 0),
    ("back", 1, 0),
    ("inter", "S", 3),
    ("back", 1, 1),
    ("inter", "V", 2),
    ("back", 0, 1),
    ("inter", "S", 0),
    ("quant", 1),
    ("inter", "S", 1),
    ("mul", 1, 1),
    ("quant", 0),
    ("mul", 1, 0),
    ("mul", 0, 1),
    ("leave", "V", 1, 1, "sync"),
    ("mul", 0, 0),
    ("leave", "V", 1, 0, "sync"),
    ("leave", "V", 0, 1, "sync"),
    ("leave", "S", 0, 0, "scalar"),
)
RING = 10
RING_V = 2


def tile_picked_hash_lin_none_sub_l_kernel(tc, xT, w_words, w_scales, offs, out):
    nc = tc.nc
    with ExitStack() as ctx:
        keep = ctx.enter_context(tc.tile_pool(name="keep", bufs=1))
        psum = ctx.enter_context(tc.psum_pool(name="psum", bufs=1))

        offsets = keep.tile([P, D * V // 16], U16, name="offsets")
        table = [keep.tile([P, T], F32, name=f"table{t}") for t in range(PACK)]
        table16 = [keep.tile([P, T], BF16, name=f"table16_{t}") for t in range(PACK)]
        picked = [[keep.tile([P, V], F32, name=f"picked{t}_{d}") for d in range(D)] for t in range(PACK)]
        spaced = keep.tile([P, RING * HALF], F32, name="spaced")
        source = {}
        whole = {}
        w_codes = keep.tile([P, N], U32, name="w_codes", align_bytes=64)
        w_scale = keep.tile([P, N], U8, name="w_scale", align_bytes=64)
        ident = keep.tile([P, P], F32, name="ident")
        warm = keep.tile([P, 8], F32, name="warm")
        warm_out = keep.tile([P, 8], F32, name="warm_out")
        sums16 = [[keep.tile([P, 2 * P], BF16, name=f"sums16_{u}_{b}") for b in range(BLOCKS)] for u in range(2)]
        x16 = [keep.tile([P, PACK * HALF], BF16, name=f"x16_{h}", align_bytes=64) for h in range(2)]
        x_codes = [keep.tile([P, HALF], U32, name=f"x_codes{h}", align_bytes=64) for h in range(2)]
        x_scale = [keep.tile([P, HALF], U8, name=f"x_scale{h}", align_bytes=64) for h in range(2)]
        result = [[keep.tile([P, HALF], F32, name=f"result{h}_{m}") for m in range(2)] for h in range(2)]
        bank = [[psum.tile([P, 4 * P], F32, name=f"bank{u}_{b}") for b in range(BLOCKS)] for u in range(2)]

        rows = xT.rearrange("(p t) c -> p t c", t=PACK)
        for t in (0, 2, 1, 3):
            for lo, hi in LOADS[t]:
                nc.sync.dma_start(out=table[t][:, lo:hi], in_=rows[:, t, lo:hi])
                if t == 0 and lo == 0:
                    nc.sync.dma_start(offsets[:], offs)

        nc.vector.memset(warm[:], 0.0)
        nc.scalar.activation(warm_out[:], warm[:], COPY)
        make_identity(nc, ident[:])
        nc.vector.memset(w_scale[:].bitcast(U32), 0)
        nc.sync.dma_start(
            out=w_codes[:].bitcast(I32), in_=w_words[0].rearrange("p n t -> p (n t)").bitcast(I32)
        )
        for q in range(4):
            nc.sync.dma_start(
                out=w_scale[32 * q : 32 * q + 4, :].bitcast(I32), in_=w_scales[0, 4 * q : 4 * q + 4, :].bitcast(I32)
            )
        nc.vector.memset(spaced[:, : RING_V * HALF], 0.0)
        nc.gpsimd.memset(spaced[:, RING_V * HALF :], 0.0)

        seen = {}

        def cast(eng, t, lo, hi):
            if eng == "V":
                nc.vector.tensor_copy(table16[t][:, lo:hi], table[t][:, lo:hi])
            elif eng == "S":
                nc.scalar.activation(table16[t][:, lo:hi], table[t][:, lo:hi], COPY)
            else:
                nc.gpsimd.tensor_scalar(table16[t][:, lo:hi], table[t][:, lo:hi], 1.0, 0.0, MULT, ADD)

        def gather(eng, t, d, lo, hi, slot):
            piece = offsets[:, (d * V + lo) // 16 : (d * V + hi) // 16]
            if eng == "V":
                nc.vector.tensor_copy(picked[t][d][:, lo:hi], table[t][:].indirect(piece))
                for b in range(lo // P, hi // P):
                    source[(t, d, b)] = picked[t][d][:, b * P : (b + 1) * P]
                for c in range(lo, hi, HALF):
                    whole[(t, d, c)] = picked[t][d][:, c : c + HALF]
            else:
                first = slot * HALF - lo
                upper = spaced[:, first + lo : first + hi].bitcast(BF16)[:, 1::2]
                nc.scalar.activation(upper, table16[t][:].indirect(piece), COPY)
                for b in range(lo // P, hi // P):
                    source[(t, d, b)] = spaced[:, first + b * P : first + (b + 1) * P]
                for c in range(lo, hi, HALF):
                    whole[(t, d, c)] = spaced[:, first + c : first + c + HALF]

        def pre(eng, t, d0, d1, lo, hi):
            both = keep.tile([P, hi - lo], F32, name=f"both{t}_{d0}_{lo}")
            nc.vector.tensor_tensor(both[:], whole[(t, d0, lo)], whole[(t, d1, lo)], ADD)
            for b in range(lo // P, hi // P):
                source[(t, f"{d0}+", b)] = both[:, b * P - lo : (b + 1) * P - lo]

        def add(t, d, b):
            count = seen.get((t, b), 0)
            seen.setdefault((t, b), 0)
            seen[(t, b)] = count + 1
            e = t % 2
            nc.tensor.matmul(
                bank[t // 2][b][:, e * P : (e + 1) * P],
                lhsT=source[(t, d, b)],
                rhs=ident[:],
                start=(count == 0),
                stop=(count == len([s for s in STEPS if s[0] == "add" and s[1] == t and s[3] == b]) - 1),
                is_transpose=True,
            )

        def copy(eng, dst, src):
            if eng == "V":
                nc.vector.tensor_copy(dst, src)
            else:
                nc.scalar.copy(dst, src)

        def round_sums(eng, u, b):
            copy(
                eng,
                sums16[u][b][:].rearrange("v (p e) -> v p e", e=2),
                bank[u][b][:, : 2 * P].rearrange("v (e p) -> v p e", e=2),
            )

        def turn_back(u, b):
            nc.tensor.transpose(bank[0][b][:, (2 + u) * P : (3 + u) * P], sums16[u][b][:].bitcast(F32), ident[:])

        def interleave(eng, b):
            h, c = divmod(b, 2)
            copy(
                eng,
                x16[h][:, c * PACK * P : (c + 1) * PACK * P].bitcast(F32).rearrange("p (v u) -> p v u", u=2),
                bank[0][b][:, 2 * P :].rearrange("p (u v) -> p v u", u=2),
            )

        def quantize(h):
            nc.vector.quantize_mx(out=x_codes[h][:].bitcast(FP8X4), scales=x_scale[h][:], in_=x16[h][:])

        def multiply(h, m):
            nc.tensor.matmul_mx(
                out=bank[1][2 * h + m][:, 2 * P :],
                lhsT=w_codes[:, m * P : (m + 1) * P].bitcast(FP8X4),
                lhsT_scale=w_scale[:, m * P : (m + 1) * P],
                rhs=x_codes[h][:].bitcast(FP8X4),
                rhs_scale=x_scale[h][:],
                start=True,
                stop=True,
            )

        def leave(eng, h, m, queue):
            copy(eng, result[h][m][:], bank[1][2 * h + m][:, 2 * P :])
            dst = out[m * P : (m + 1) * P, h * HALF : (h + 1) * HALF]
            if queue == "sync":
                nc.sync.dma_start(out=dst, in_=result[h][m][:])
            else:
                nc.scalar.dma_start(out=dst, in_=result[h][m][:])

        calls = {
            "cast": cast,
            "gather": gather,
            "add": add,
            "pre": pre,
            "round": round_sums,
            "back": turn_back,
            "inter": interleave,
            "quant": quantize,
            "mul": multiply,
            "leave": leave,
        }
        for step in STEPS:
            calls[step[0]](*step[1:])
